import numpy as np
import ml_dtypes


def mxq(x, axis, fmt="e4m3"):
    dtype, down = {"e4m3": (ml_dtypes.float8_e4m3fn, 7), "e5m2": (ml_dtypes.float8_e5m2, 14)}[fmt]
    v = np.moveaxis(np.asarray(x, np.float32).astype(ml_dtypes.bfloat16).astype(np.float64), axis, -1)
    blocks = v.reshape(v.shape[:-1] + (-1, 32))
    amax = np.abs(blocks).max(-1, keepdims=True)
    byte = np.maximum(np.where(amax > 0, np.frexp(amax)[1] - 1 + 127, 0) - down, 1)
    scale = np.exp2(byte - 127.0)
    codes = (blocks / scale).astype(np.float32).astype(dtype).astype(np.float64)
    return np.moveaxis((codes * scale).reshape(v.shape), -1, axis)


WIDE = False


def mx_kscale(k):
    if not WIDE:
        return np.ones(k)
    levels = np.array([10, -10, 5, -5, 0])
    if k % 512:
        return np.exp2(np.random.permutation(np.resize(levels, k // 32))).repeat(32)
    a = np.empty((k // 512, 16))
    for p in range(k // 512):
        a[p, :8] = np.random.permutation(np.resize(levels, 8))
        for g in range(8):
            far = levels[np.abs(levels - a[p, g]) >= 10]
            a[p, g + 8] = far[np.random.randint(len(far))]
    return np.exp2(a.ravel()).repeat(32)


def f64(x):
    return np.asarray(x).astype(np.float64)


def striped(idx):
    return np.tile(idx.reshape(-1, 16).T, (8, 1)).astype(np.uint16)


def unstriped(offs):
    return offs[:16].T.reshape(-1).astype(np.int64)


def pack_weight(w):
    k, n = w.shape
    w = f64(np.asarray(w, np.float32).astype(ml_dtypes.bfloat16)).reshape(k // 32, 32, n)
    amax = np.abs(w).max(1)
    byte = np.clip(np.where(amax > 0, np.frexp(amax)[1] - 1 + 127 - 7, 1), 1, 254)
    scaled = (w * np.exp2(127.0 - byte)[:, None, :]).reshape(k, n).astype(np.float32)
    words = np.ascontiguousarray(scaled.reshape(k // 512, 128, 4, n).transpose(0, 1, 3, 2)).astype(ml_dtypes.float8_e4m3fn).view(np.uint8)
    return words, np.ascontiguousarray(byte.astype(np.uint8).reshape(k // 512, 16, n))


def unpack_weight(words, scales):
    g, p, n, _ = words.shape
    vals = np.ascontiguousarray(words).view(ml_dtypes.float8_e4m3fn).astype(np.float64) * np.repeat(np.exp2(scales.astype(np.float64) - 127.0), 8, axis=1)[..., None]
    return vals.transpose(0, 1, 3, 2).reshape(g * 512, n)


def planes(y):
    n, m = y.shape
    v = y.astype(np.float32).astype(ml_dtypes.bfloat16).astype(np.float64).reshape(n // 32, 32, m)
    top = np.abs(v).max(1)
    byte = np.clip(np.where(top > 0, np.frexp(top)[1] - 1 + 127 - 7, 1), 1, 254)
    codes = (v * np.exp2(127.0 - byte)[:, None, :]).reshape(n, m).astype(np.float32).astype(ml_dtypes.float8_e4m3fn).view(np.uint8)
    words = codes.reshape(n // 512, 128, 4, m).transpose(0, 1, 3, 2)
    return np.ascontiguousarray(words), np.ascontiguousarray(byte.astype(np.uint8).reshape(n // 512, 16, m))


def relu(v):
    return np.maximum(v, 0.0)


def sigmoid(v):
    return 1.0 / (1.0 + np.exp(-np.maximum(v, -700.0)))


K, T, S, H, N = 512, 1024, 512, 512, 512


def setup_inputs():
    n = np.random.standard_normal
    s = mx_kscale(K)[:, None]
    u = mx_kscale(H)
    packed_xT = pack_weight(n((K, T)) * s)
    return {
        "x_words": packed_xT[0],
        "x_scales": packed_xT[1],
        "w1": (n((K, N)) / np.sqrt(2 * K) / s).astype(np.float32),
        "w2": (n((K, N)) / np.sqrt(2 * K) / s).astype(np.float32),
        "w3": (n((K, H)) / np.sqrt(2 * K) / s * u).astype(np.float32),
        "w4": (n((K, H)) / np.sqrt(2 * K) / s * u).astype(np.float32),
        "w5": (n((H, N)) / np.sqrt(H) / u[:, None]).astype(np.float32),
        "offs": striped(np.random.permutation(T)[:S]),
        "prev": striped(np.random.permutation(T)[:S]),
    }


def reference(x_words, x_scales, w1, w2, w3, w4, w5, offs, prev):
    xq = unpack_weight(x_words, x_scales)[:, unstriped(offs)]
    x_prev = unpack_weight(x_words, x_scales)[:, unstriped(prev)]
    h = relu(mxq(f64(w3), 0, "e4m3").T @ xq + mxq(f64(w4), 0, "e4m3").T @ x_prev)
    y = mxq(f64(w5), 0, "e4m3").T @ mxq(h, 0, "e4m3")
    r = sigmoid(mxq(f64(w1), 0, "e4m3").T @ xq + mxq(f64(w2), 0, "e4m3").T @ x_prev)
    out_0 = y * r
    return (out_0,) + planes(out_0)

@@ -1,0 +1,158 @@
+from contextlib import ExitStack
+
+import concourse.mybir as mybir
+
+K, T, S, H, N = 512, 1024, 512, 512, 512
+FLOPS = 5 * 2 * 512 * 512 * 512
+
+F32 = mybir.dt.float32
+BF16 = mybir.dt.bfloat16
+I32 = mybir.dt.int32
+U32 = mybir.dt.uint32
+U16 = mybir.dt.uint16
+U8 = mybir.dt.uint8
+FP8X4 = mybir.dt.float8_e4m3fn_x4
+ACT = mybir.ActivationFunctionType
+ALU = mybir.AluOpType
+
+P = 128
+PACK = 4
+HALF = 64
+CHUNK = 128
+CHUNKS = S // CHUNK
+
+
+def tile_picked_zshift_relu_po_kernel(tc, x_words, x_scales, w1, w2, w3, w4, w5, offs, prev, out_0, out_1, out_2):
+    nc = tc.nc
+    with ExitStack() as ctx:
+        keep = ctx.enter_context(tc.tile_pool(name="keep", bufs=1))
+        psum = ctx.enter_context(tc.psum_pool(name="psum", bufs=1))
+
+        offs_sb = keep.tile([P, S // 16], U16, name="offs_sb")
+        prev_sb = keep.tile([P, S // 16], U16, name="prev_sb")
+        table_words = keep.tile([P, T], I32, name="table_words", align_bytes=64)
+        table_scales = keep.tile([P, T], U8, name="table_scales", align_bytes=64)
+
+        nc.vector.memset(table_scales[:].bitcast(I32), 0)
+        nc.sync.dma_start(offs_sb[:], offs)
+        nc.sync.dma_start(table_words[:], x_words[0].rearrange("p c r -> p (c r)").bitcast(I32))
+        nc.sync.dma_start(prev_sb[:], prev)
+        for q in range(4):
+            nc.scalar.dma_start(table_scales[32 * q : 32 * q + 4, :].bitcast(I32), x_scales[0, 4 * q : 4 * q + 4, :].bitcast(I32))
+        warm = keep.tile([P, 8], F32, name="warm")
+        warm_out = keep.tile([P, 8], F32, name="warm_out")
+        nc.vector.memset(warm[:], 0.0)
+        nc.scalar.activation(warm_out[:], warm[:], ACT.Sigmoid)
+
+        weights = {"w3": w3, "w4": w4, "w1": w1, "w2": w2, "w5": w5}
+        raw = {}
+        for name, w in weights.items():
+            rows = w.rearrange("(p j) m -> p j m", j=PACK)
+            for half in range(2):
+                raw[name, half] = keep.tile([P, PACK, 256], F32, name=f"raw_{name}_{half}", align_bytes=64)
+                nc.sync.dma_start(raw[name, half][:], rows[:, :, 256 * half : 256 * half + 256])
+
+        picked = {}
+        for name, lst in (("now", offs_sb), ("prev", prev_sb)):
+            words = keep.tile([P, S], U32, name=f"words_{name}", align_bytes=64)
+            nc.vector.tensor_copy(words[:], table_words[:].bitcast(U32).indirect(lst[:]))
+            picked[name] = [words]
+        for name, lst in (("now", offs_sb), ("prev", prev_sb)):
+            scales = keep.tile([P, S], U8, name=f"scales_{name}", align_bytes=64)
+            nc.vector.tensor_copy(scales[:], table_scales[:].indirect(lst[:]))
+            picked[name].append(scales)
+
+        rounded = {name: keep.tile([P, 2048], BF16, name=f"bf_{name}", align_bytes=64) for name in weights}
+        codes = {name: keep.tile([P, 512], U32, name=f"codes_{name}", align_bytes=64) for name in weights}
+        scales = {name: keep.tile([P, 512], U8, name=f"sc_{name}", align_bytes=64) for name in weights}
+
+        def cast(engine, name, half, t0=0, t1=PACK):
+            src = raw[name, half][:].rearrange("p j (m t) -> p m j t", t=PACK)[:, :, :, t0:t1]
+            dst = rounded[name][:].rearrange("p (t m j) -> p m j t", t=PACK, j=PACK)[:, HALF * half : HALF * half + HALF, :, t0:t1]
+            if engine == "scalar":
+                nc.scalar.copy(dst, src)
+            else:
+                nc.vector.tensor_copy(dst, src)
+
+        def quant(name):
+            nc.vector.quantize_mx(out=codes[name][:].bitcast(FP8X4), scales=scales[name][:], in_=rounded[name][:])
+
+        def product(out, name, t, rhs, rhs_scale, start, stop):
+            cols = slice(P * t, P * t + P)
+            nc.tensor.matmul_mx(out=out, lhsT=codes[name][:, cols].bitcast(FP8X4), lhsT_scale=scales[name][:, cols],
+                                rhs=rhs.bitcast(FP8X4), rhs_scale=rhs_scale, start=start, stop=stop)
+
+        cast("scalar", "w3", 0)
+        cast("scalar", "w3", 1)
+        cast("scalar", "w4", 0)
+        quant("w3")
+        cast("vector", "w4", 1, 0, 2)
+        cast("scalar", "w4", 1, 2, 4)
+        quant("w4")
+        cast("scalar", "w1", 0)
+        cast("vector", "w1", 1)
+        quant("w1")
+
+        h_bf = keep.tile([P, S * PACK], BF16, name="h_bf", align_bytes=64)
+        h_codes = keep.tile([P, S], U32, name="h_codes", align_bytes=64)
+        h_scales = keep.tile([P, S], U8, name="h_scales", align_bytes=64)
+        for c in range(CHUNKS):
+            tok = slice(CHUNK * c, CHUNK * c + CHUNK)
+            bank = psum.tile([P, PACK, CHUNK], F32, name=f"h_bank{c}", tag=f"chunk{c}")
+            for t in range(PACK):
+                product(bank[:, t, :], "w3", t, picked["now"][0][:, tok], picked["now"][1][:, tok], True, False)
+                product(bank[:, t, :], "w4", t, picked["prev"][0][:, tok], picked["prev"][1][:, tok], False, True)
+            nc.scalar.activation(h_bf[:, 512 * c : 512 * c + 512].rearrange("p (n t) -> p n t", t=PACK),
+                                 bank[:].rearrange("p t n -> p n t"), ACT.Relu)
+
+        z_banks = [psum.tile([P, S], F32, name=f"z_bank{t}", tag=f"z{t}") for t in range(PACK)]
+        for t in range(PACK):
+            product(z_banks[t][:], "w1", t, picked["now"][0][:], picked["now"][1][:], True, False)
+        cast("vector", "w2", 0)
+        cast("vector", "w2", 1)
+        quant("w2")
+        for t in range(PACK):
+            product(z_banks[t][:], "w2", t, picked["prev"][0][:], picked["prev"][1][:], False, True)
+        cast("scalar", "w5", 0)
+        for g in range(2):
+            nc.vector.quantize_mx(out=h_codes[:, 256 * g : 256 * g + 256].bitcast(FP8X4), scales=h_scales[:, 256 * g : 256 * g + 256],
+                                  in_=h_bf[:, 1024 * g : 1024 * g + 1024])
+        cast("vector", "w5", 1)
+        quant("w5")
+
+        gate = [keep.tile([P, PACK, 256], F32, name=f"gate{g}", align_bytes=64) for g in range(2)]
+        for g in range(2):
+            for t in range(PACK):
+                nc.scalar.activation(gate[g][:, t, :], z_banks[t][:, 256 * g : 256 * g + 256], ACT.Sigmoid)
+
+        out_rows = out_0.rearrange("(p t) n -> p t n", t=PACK)
+        out_words = out_1[0].rearrange("p c r -> p (c r)").bitcast(I32)
+        o_codes = keep.tile([P, S], U32, name="o_codes", align_bytes=64)
+        o_scales = keep.tile([P, S], U8, name="o_scales", align_bytes=64)
+        result = [keep.tile([P, PACK, CHUNK], F32, name=f"result{c}", align_bytes=64) for c in range(CHUNKS)]
+        result_bf = [keep.tile([P, CHUNK * PACK], BF16, name=f"result_bf{c}", align_bytes=64) for c in range(CHUNKS)]
+        for c in range(CHUNKS):
+            tok = slice(CHUNK * c, CHUNK * c + CHUNK)
+            bank = psum.tile([P, PACK, CHUNK], F32, name=f"y_bank{c}", tag=f"chunk{c}")
+            for t in range(PACK):
+                product(bank[:, t, :], "w5", t, h_codes[:, tok], h_scales[:, tok], True, True)
+            lo = CHUNK * (c % 2)
+            nc.vector.tensor_tensor(result[c][:], bank[:], gate[c // 2][:, :, lo : lo + CHUNK], ALU.mult)
+            nc.sync.dma_start(out_rows[:, :, tok], result[c][:])
+        for c in range(CHUNKS):
+            tok = slice(CHUNK * c, CHUNK * c + CHUNK)
+            src = result[c][:].rearrange("p t (a i) -> p a t i", i=4)
+            dst = result_bf[c][:].rearrange("p (a i t) -> p a t i", i=4, t=PACK)
+            if c < 3:
+                nc.scalar.copy(dst, src)
+            else:
+                nc.vector.tensor_copy(dst, src)
+        for c in range(CHUNKS):
+            tok = slice(CHUNK * c, CHUNK * c + CHUNK)
+            nc.vector.quantize_mx(out=o_codes[:, tok].bitcast(FP8X4), scales=o_scales[:, tok], in_=result_bf[c][:])
+            if c % 2 == 1:
+                both = slice(CHUNK * (c - 1), CHUNK * (c + 1))
+                nc.sync.dma_start(out_words[:, both], o_codes[:, both].bitcast(I32))
+        for q in range(4):
+            queue = nc.sync if q % 2 == 0 else nc.scalar
+            queue.dma_start(out_2[0, 4 * q : 4 * q + 4, :].bitcast(I32), o_scales[32 * q : 32 * q + 4, :].bitcast(I32))

@@ -17,9 +17,9 @@ ALU = mybir.AluOpType
 
 P = 128
 PACK = 4
-HALF = 64
 CHUNK = 128
-CHUNKS = S // CHUNK
+HALF = S // 2
+SCALAR_TAIL = 64
 
 
 def tile_picked_zshift_relu_po_kernel(tc, x_words, x_scales, w1, w2, w3, w4, w5, offs, prev, out_0, out_1, out_2):
@@ -34,11 +34,11 @@ def tile_picked_zshift_relu_po_kernel(tc, x_words, x_scales, w1, w2, w3, w4, w5,
         table_scales = keep.tile([P, T], U8, name="table_scales", align_bytes=64)
 
         nc.vector.memset(table_scales[:].bitcast(I32), 0)
-        nc.sync.dma_start(offs_sb[:], offs)
         nc.sync.dma_start(table_words[:], x_words[0].rearrange("p c r -> p (c r)").bitcast(I32))
+        nc.sync.dma_start(offs_sb[:], offs)
+        for r in range(4):
+            nc.sync.dma_start(table_scales[r:P:32, :].bitcast(I32), x_scales[0, r:16:4, :].bitcast(I32))
         nc.sync.dma_start(prev_sb[:], prev)
-        for q in range(4):
-            nc.scalar.dma_start(table_scales[32 * q : 32 * q + 4, :].bitcast(I32), x_scales[0, 4 * q : 4 * q + 4, :].bitcast(I32))
         warm = keep.tile([P, 8], F32, name="warm")
         warm_out = keep.tile([P, 8], F32, name="warm_out")
         nc.vector.memset(warm[:], 0.0)
@@ -47,112 +47,112 @@ def tile_picked_zshift_relu_po_kernel(tc, x_words, x_scales, w1, w2, w3, w4, w5,
         weights = {"w3": w3, "w4": w4, "w1": w1, "w2": w2, "w5": w5}
         raw = {}
         for name, w in weights.items():
-            rows = w.rearrange("(p j) m -> p j m", j=PACK)
-            for half in range(2):
-                raw[name, half] = keep.tile([P, PACK, 256], F32, name=f"raw_{name}_{half}", align_bytes=64)
-                nc.sync.dma_start(raw[name, half][:], rows[:, :, 256 * half : 256 * half + 256])
+            raw[name] = keep.tile([P, PACK, N], F32, name=f"raw_{name}", tag=f"raw_{name}", align_bytes=64)
+            nc.sync.dma_start(raw[name][:], w.rearrange("(p j) m -> p j m", j=PACK))
 
-        picked = {}
+        words, scales = {}, {}
         for name, lst in (("now", offs_sb), ("prev", prev_sb)):
-            words = keep.tile([P, S], U32, name=f"words_{name}", align_bytes=64)
-            nc.vector.tensor_copy(words[:], table_words[:].bitcast(U32).indirect(lst[:]))
-            picked[name] = [words]
+            words[name] = keep.tile([P, S], U32, name=f"words_{name}", align_bytes=64)
+            nc.vector.tensor_copy(words[name][:], table_words[:].bitcast(U32).indirect(lst[:]))
         for name, lst in (("now", offs_sb), ("prev", prev_sb)):
-            scales = keep.tile([P, S], U8, name=f"scales_{name}", align_bytes=64)
-            nc.vector.tensor_copy(scales[:], table_scales[:].indirect(lst[:]))
-            picked[name].append(scales)
+            scales[name] = keep.tile([P, S], U8, name=f"scales_{name}", align_bytes=64)
+            nc.vector.tensor_copy(scales[name][:], table_scales[:].indirect(lst[:]))
 
-        rounded = {name: keep.tile([P, 2048], BF16, name=f"bf_{name}", align_bytes=64) for name in weights}
-        codes = {name: keep.tile([P, 512], U32, name=f"codes_{name}", align_bytes=64) for name in weights}
-        scales = {name: keep.tile([P, 512], U8, name=f"sc_{name}", align_bytes=64) for name in weights}
+        rounded = {}
+        for name in weights:
+            rounded[name] = keep.tile([P, PACK * N], BF16, name=f"rounded_{name}", align_bytes=64)
+            words[name] = keep.tile([P, N], U32, name=f"words_{name}", align_bytes=64)
+            scales[name] = keep.tile([P, N], U8, name=f"scales_{name}", align_bytes=64)
 
-        def cast(engine, name, half, t0=0, t1=PACK):
-            src = raw[name, half][:].rearrange("p j (m t) -> p m j t", t=PACK)[:, :, :, t0:t1]
-            dst = rounded[name][:].rearrange("p (t m j) -> p m j t", t=PACK, j=PACK)[:, HALF * half : HALF * half + HALF, :, t0:t1]
-            if engine == "scalar":
-                nc.scalar.copy(dst, src)
-            else:
-                nc.vector.tensor_copy(dst, src)
+        def round_weight(copy, name, u0, u1):
+            src = raw[name][:].rearrange("p j (m u e) -> p u m j e", u=2, e=2)[:, u0:u1]
+            dst = rounded[name][:].rearrange("p (u e m j) -> p u m j e", u=2, e=2, j=PACK)[:, u0:u1]
+            copy(dst, src)
 
-        def quant(name):
-            nc.vector.quantize_mx(out=codes[name][:].bitcast(FP8X4), scales=scales[name][:], in_=rounded[name][:])
+        def quantize(name, source, first, count):
+            cols = slice(first, first + count)
+            nc.vector.quantize_mx(out=words[name][:, cols].bitcast(FP8X4), scales=scales[name][:, cols],
+                                  in_=source[:, PACK * first : PACK * (first + count)])
 
-        def product(out, name, t, rhs, rhs_scale, start, stop):
+        def product(out, weight, t, moving, tokens, start, stop):
             cols = slice(P * t, P * t + P)
-            nc.tensor.matmul_mx(out=out, lhsT=codes[name][:, cols].bitcast(FP8X4), lhsT_scale=scales[name][:, cols],
-                                rhs=rhs.bitcast(FP8X4), rhs_scale=rhs_scale, start=start, stop=stop)
+            nc.tensor.matmul_mx(out=out, lhsT=words[weight][:, cols].bitcast(FP8X4), lhsT_scale=scales[weight][:, cols],
+                                rhs=words[moving][:, tokens].bitcast(FP8X4), rhs_scale=scales[moving][:, tokens], start=start, stop=stop)
 
-        cast("scalar", "w3", 0)
-        cast("scalar", "w3", 1)
-        cast("scalar", "w4", 0)
-        quant("w3")
-        cast("vector", "w4", 1, 0, 2)
-        cast("scalar", "w4", 1, 2, 4)
-        quant("w4")
-        cast("scalar", "w1", 0)
-        cast("vector", "w1", 1)
-        quant("w1")
+        on_scalar, on_vector = nc.scalar.copy, nc.vector.tensor_copy
+        everyone = slice(0, S)
 
-        h_bf = keep.tile([P, S * PACK], BF16, name="h_bf", align_bytes=64)
-        h_codes = keep.tile([P, S], U32, name="h_codes", align_bytes=64)
-        h_scales = keep.tile([P, S], U8, name="h_scales", align_bytes=64)
-        for c in range(CHUNKS):
-            tok = slice(CHUNK * c, CHUNK * c + CHUNK)
-            bank = psum.tile([P, PACK, CHUNK], F32, name=f"h_bank{c}", tag=f"chunk{c}")
+        for name in ("w3", "w4", "w1"):
+            round_weight(on_scalar, name, 1, 2)
+            round_weight(on_vector, name, 0, 1)
+            if name == "w3":
+                quantize(name, rounded[name], N // 2, N // 2)
+                quantize(name, rounded[name], 0, N // 2)
+            else:
+                quantize(name, rounded[name], 0, N)
+            if name == "w3":
+                warm_bank = psum.tile([P, S], F32, name="warm_bank", tag="z0")
+                for i in range(3):
+                    product(warm_bank[:], "w3", 0, "now", everyone, True, True)
+
+        h_rounded = keep.tile([P, S * PACK], BF16, name="h_rounded", tag="raw_w1", align_bytes=64)
+        for c in range(S // CHUNK):
+            tokens = slice(CHUNK * c, CHUNK * c + CHUNK)
+            bank = psum.tile([P, PACK, CHUNK], F32, name=f"h_bank{c}", tag=f"hy{c}")
             for t in range(PACK):
-                product(bank[:, t, :], "w3", t, picked["now"][0][:, tok], picked["now"][1][:, tok], True, False)
-                product(bank[:, t, :], "w4", t, picked["prev"][0][:, tok], picked["prev"][1][:, tok], False, True)
-            nc.scalar.activation(h_bf[:, 512 * c : 512 * c + 512].rearrange("p (n t) -> p n t", t=PACK),
+                product(bank[:, t, :], "w3", t, "now", tokens, True, False)
+                product(bank[:, t, :], "w4", t, "prev", tokens, False, True)
+            nc.scalar.activation(h_rounded[:, PACK * CHUNK * c : PACK * CHUNK * (c + 1)].rearrange("p (n t) -> p n t", t=PACK),
                                  bank[:].rearrange("p t n -> p n t"), ACT.Relu)
 
         z_banks = [psum.tile([P, S], F32, name=f"z_bank{t}", tag=f"z{t}") for t in range(PACK)]
         for t in range(PACK):
-            product(z_banks[t][:], "w1", t, picked["now"][0][:], picked["now"][1][:], True, False)
-        cast("vector", "w2", 0)
-        cast("vector", "w2", 1)
-        quant("w2")
+            product(z_banks[t][:], "w1", t, "now", everyone, True, False)
+
+        round_weight(on_vector, "w2", 0, 1)
+        round_weight(on_vector, "w2", 1, 2)
+        words["h"] = keep.tile([P, S], U32, name="words_h", tag="raw_w2", align_bytes=64)
+        scales["h"] = keep.tile([P, S], U8, name="scales_h", align_bytes=64)
+        quantize("w2", rounded["w2"], 0, N // 2)
+        quantize("h", h_rounded, 0, HALF)
+        quantize("w2", rounded["w2"], N // 2, N // 2)
+        quantize("h", h_rounded, HALF, HALF)
         for t in range(PACK):
-            product(z_banks[t][:], "w2", t, picked["prev"][0][:], picked["prev"][1][:], False, True)
-        cast("scalar", "w5", 0)
-        for g in range(2):
-            nc.vector.quantize_mx(out=h_codes[:, 256 * g : 256 * g + 256].bitcast(FP8X4), scales=h_scales[:, 256 * g : 256 * g + 256],
-                                  in_=h_bf[:, 1024 * g : 1024 * g + 1024])
-        cast("vector", "w5", 1)
-        quant("w5")
+            product(z_banks[t][:], "w2", t, "prev", everyone, False, True)
 
-        gate = [keep.tile([P, PACK, 256], F32, name=f"gate{g}", align_bytes=64) for g in range(2)]
-        for g in range(2):
-            for t in range(PACK):
-                nc.scalar.activation(gate[g][:, t, :], z_banks[t][:, 256 * g : 256 * g + 256], ACT.Sigmoid)
+        round_weight(on_scalar, "w5", 1, 2)
+        round_weight(on_vector, "w5", 0, 1)
+        quantize("w5", rounded["w5"], 0, N // 2)
+        quantize("w5", rounded["w5"], N // 2, N // 2)
 
+        gate = keep.tile([P, PACK, S], F32, name="gate", tag="raw_w5", align_bytes=64)
+        result = keep.tile([P, PACK, S], F32, name="result", align_bytes=64)
         out_rows = out_0.rearrange("(p t) n -> p t n", t=PACK)
+        for t in range(PACK):
+            nc.scalar.activation(gate[:, t, :], z_banks[t][:], ACT.Sigmoid)
+            bank = psum.tile([P, S], F32, name=f"y_bank{t}", tag=f"hy{t}")
+            product(bank[:], "w5", t, "h", everyone, True, True)
+            for tokens in ([everyone] if t < PACK - 1 else [slice(0, HALF), slice(HALF, S)]):
+                nc.vector.tensor_tensor(result[:, t, tokens], bank[:, tokens], gate[:, t, tokens], ALU.mult)
+            nc.sync.dma_start(out_rows[:, t, :], result[:, t, :])
+
+        result_rounded = keep.tile([P, S * PACK], BF16, name="result_rounded", align_bytes=64)
+        words["out"] = keep.tile([P, S], U32, name="words_out", align_bytes=64)
+        scales["out"] = keep.tile([P, S], U8, name="scales_out", align_bytes=64)
+
+        def round_result(copy, first, last):
+            src = result[:, :, first:last].rearrange("p t (a i) -> p a t i", i=4)
+            dst = result_rounded[:, PACK * first : PACK * last].rearrange("p (a i t) -> p a t i", i=4, t=PACK)
+            copy(dst, src)
+
+        round_result(on_scalar, 0, CHUNK)
+        round_result(on_vector, CHUNK, HALF)
+        round_result(on_vector, HALF, S - SCALAR_TAIL)
+        round_result(on_scalar, S - SCALAR_TAIL, S)
         out_words = out_1[0].rearrange("p c r -> p (c r)").bitcast(I32)
-        o_codes = keep.tile([P, S], U32, name="o_codes", align_bytes=64)
-        o_scales = keep.tile([P, S], U8, name="o_scales", align_bytes=64)
-        result = [keep.tile([P, PACK, CHUNK], F32, name=f"result{c}", align_bytes=64) for c in range(CHUNKS)]
-        result_bf = [keep.tile([P, CHUNK * PACK], BF16, name=f"result_bf{c}", align_bytes=64) for c in range(CHUNKS)]
-        for c in range(CHUNKS):
-            tok = slice(CHUNK * c, CHUNK * c + CHUNK)
-            bank = psum.tile([P, PACK, CHUNK], F32, name=f"y_bank{c}", tag=f"chunk{c}")
-            for t in range(PACK):
-                product(bank[:, t, :], "w5", t, h_codes[:, tok], h_scales[:, tok], True, True)
-            lo = CHUNK * (c % 2)
-            nc.vector.tensor_tensor(result[c][:], bank[:], gate[c // 2][:, :, lo : lo + CHUNK], ALU.mult)
-            nc.sync.dma_start(out_rows[:, :, tok], result[c][:])
-        for c in range(CHUNKS):
-            tok = slice(CHUNK * c, CHUNK * c + CHUNK)
-            src = result[c][:].rearrange("p t (a i) -> p a t i", i=4)
-            dst = result_bf[c][:].rearrange("p (a i t) -> p a t i", i=4, t=PACK)
-            if c < 3:
-                nc.scalar.copy(dst, src)
-            else:
-                nc.vector.tensor_copy(dst, src)
-        for c in range(CHUNKS):
-            tok = slice(CHUNK * c, CHUNK * c + CHUNK)
-            nc.vector.quantize_mx(out=o_codes[:, tok].bitcast(FP8X4), scales=o_scales[:, tok], in_=result_bf[c][:])
-            if c % 2 == 1:
-                both = slice(CHUNK * (c - 1), CHUNK * (c + 1))
-                nc.sync.dma_start(out_words[:, both], o_codes[:, both].bitcast(I32))
-        for q in range(4):
-            queue = nc.sync if q % 2 == 0 else nc.scalar
-            queue.dma_start(out_2[0, 4 * q : 4 * q + 4, :].bitcast(I32), o_scales[32 * q : 32 * q + 4, :].bitcast(I32))
+        for first in (0, HALF):
+            quantize("out", result_rounded, first, HALF)
+            nc.sync.dma_start(out_words[:, first : first + HALF], words["out"][:, first : first + HALF].bitcast(I32))
+        for r in range(4):
+            queue = nc.sync if r % 2 == 0 else nc.scalar
+            queue.dma_start(out_2[0, r:16:4, :].bitcast(I32), scales["out"][r:P:32, :].bitcast(I32))

@@ -2,7 +2,7 @@ from contextlib import ExitStack
 
 import concourse.mybir as mybir
 
-K, T, S, H, N = 512, 1024, 512, 512, 512
+T, S, N = 1024, 512, 512
 FLOPS = 5 * 2 * 512 * 512 * 512
 
 F32 = mybir.dt.float32
@@ -17,6 +17,8 @@ ALU = mybir.AluOpType
 
 P = 128
 PACK = 4
+QUADRANT = 32
+SCALE_ROWS = 16
 CHUNK = 128
 HALF = S // 2
 SCALAR_TAIL = 64
@@ -32,17 +34,17 @@ def tile_picked_zshift_relu_po_kernel(tc, x_words, x_scales, w1, w2, w3, w4, w5,
         prev_sb = keep.tile([P, S // 16], U16, name="prev_sb")
         table_words = keep.tile([P, T], I32, name="table_words", align_bytes=64)
         table_scales = keep.tile([P, T], U8, name="table_scales", align_bytes=64)
-
         nc.vector.memset(table_scales[:].bitcast(I32), 0)
         nc.sync.dma_start(table_words[:], x_words[0].rearrange("p c r -> p (c r)").bitcast(I32))
         nc.sync.dma_start(offs_sb[:], offs)
-        for r in range(4):
-            nc.sync.dma_start(table_scales[r:P:32, :].bitcast(I32), x_scales[0, r:16:4, :].bitcast(I32))
+        for r in range(PACK):
+            nc.sync.dma_start(table_scales[r:P:QUADRANT, :].bitcast(I32), x_scales[0, r:SCALE_ROWS:PACK, :].bitcast(I32))
         nc.sync.dma_start(prev_sb[:], prev)
-        warm = keep.tile([P, 8], F32, name="warm")
-        warm_out = keep.tile([P, 8], F32, name="warm_out")
-        nc.vector.memset(warm[:], 0.0)
-        nc.scalar.activation(warm_out[:], warm[:], ACT.Sigmoid)
+
+        preload_in = keep.tile([P, 8], F32, name="preload_in")
+        preload_out = keep.tile([P, 8], F32, name="preload_out")
+        nc.vector.memset(preload_in[:], 0.0)
+        nc.scalar.activation(preload_out[:], preload_in[:], ACT.Sigmoid)
 
         weights = {"w3": w3, "w4": w4, "w1": w1, "w2": w2, "w5": w5}
         raw = {}
@@ -51,12 +53,12 @@ def tile_picked_zshift_relu_po_kernel(tc, x_words, x_scales, w1, w2, w3, w4, w5,
             nc.sync.dma_start(raw[name][:], w.rearrange("(p j) m -> p j m", j=PACK))
 
         words, scales = {}, {}
-        for name, lst in (("now", offs_sb), ("prev", prev_sb)):
+        for name, offsets in (("now", offs_sb), ("prev", prev_sb)):
             words[name] = keep.tile([P, S], U32, name=f"words_{name}", align_bytes=64)
-            nc.vector.tensor_copy(words[name][:], table_words[:].bitcast(U32).indirect(lst[:]))
-        for name, lst in (("now", offs_sb), ("prev", prev_sb)):
+            nc.vector.tensor_copy(words[name][:], table_words[:].bitcast(U32).indirect(offsets[:]))
+        for name, offsets in (("now", offs_sb), ("prev", prev_sb)):
             scales[name] = keep.tile([P, S], U8, name=f"scales_{name}", align_bytes=64)
-            nc.vector.tensor_copy(scales[name][:], table_scales[:].indirect(lst[:]))
+            nc.vector.tensor_copy(scales[name][:], table_scales[:].indirect(offsets[:]))
 
         rounded = {}
         for name in weights:
@@ -64,76 +66,88 @@ def tile_picked_zshift_relu_po_kernel(tc, x_words, x_scales, w1, w2, w3, w4, w5,
             words[name] = keep.tile([P, N], U32, name=f"words_{name}", align_bytes=64)
             scales[name] = keep.tile([P, N], U8, name=f"scales_{name}", align_bytes=64)
 
-        def round_weight(copy, name, u0, u1):
-            src = raw[name][:].rearrange("p j (m u e) -> p u m j e", u=2, e=2)[:, u0:u1]
-            dst = rounded[name][:].rearrange("p (u e m j) -> p u m j e", u=2, e=2, j=PACK)[:, u0:u1]
+        def round_weight(copy, name, u):
+            src = raw[name][:].rearrange("p j (m u e) -> p u m j e", u=2, e=2)[:, u : u + 1]
+            dst = rounded[name][:].rearrange("p (u e m j) -> p u m j e", u=2, e=2, j=PACK)[:, u : u + 1]
             copy(dst, src)
 
         def quantize(name, source, first, count):
             cols = slice(first, first + count)
-            nc.vector.quantize_mx(out=words[name][:, cols].bitcast(FP8X4), scales=scales[name][:, cols],
-                                  in_=source[:, PACK * first : PACK * (first + count)])
+            nc.vector.quantize_mx(
+                out=words[name][:, cols].bitcast(FP8X4),
+                scales=scales[name][:, cols],
+                in_=source[:, PACK * first : PACK * (first + count)],
+            )
 
         def product(out, weight, t, moving, tokens, start, stop):
             cols = slice(P * t, P * t + P)
-            nc.tensor.matmul_mx(out=out, lhsT=words[weight][:, cols].bitcast(FP8X4), lhsT_scale=scales[weight][:, cols],
-                                rhs=words[moving][:, tokens].bitcast(FP8X4), rhs_scale=scales[moving][:, tokens], start=start, stop=stop)
+            nc.tensor.matmul_mx(
+                out=out,
+                lhsT=words[weight][:, cols].bitcast(FP8X4),
+                lhsT_scale=scales[weight][:, cols],
+                rhs=words[moving][:, tokens].bitcast(FP8X4),
+                rhs_scale=scales[moving][:, tokens],
+                start=start,
+                stop=stop,
+            )
 
         on_scalar, on_vector = nc.scalar.copy, nc.vector.tensor_copy
-        everyone = slice(0, S)
+        all_tokens = slice(0, S)
+        pair = N // 2
 
-        for name in ("w3", "w4", "w1"):
-            round_weight(on_scalar, name, 1, 2)
-            round_weight(on_vector, name, 0, 1)
-            if name == "w3":
-                quantize(name, rounded[name], N // 2, N // 2)
-                quantize(name, rounded[name], 0, N // 2)
-            else:
-                quantize(name, rounded[name], 0, N)
-            if name == "w3":
-                warm_bank = psum.tile([P, S], F32, name="warm_bank", tag="z0")
-                for i in range(3):
-                    product(warm_bank[:], "w3", 0, "now", everyone, True, True)
+        round_weight(on_scalar, "w3", 1)
+        round_weight(on_scalar, "w3", 0)
+        quantize("w3", rounded["w3"], pair, pair)
+        quantize("w3", rounded["w3"], 0, pair)
+        for name in ("w4", "w1"):
+            round_weight(on_scalar, name, 1)
+            round_weight(on_vector, name, 0)
+            quantize(name, rounded[name], 0, N)
 
         h_rounded = keep.tile([P, S * PACK], BF16, name="h_rounded", tag="raw_w1", align_bytes=64)
         for c in range(S // CHUNK):
             tokens = slice(CHUNK * c, CHUNK * c + CHUNK)
-            bank = psum.tile([P, PACK, CHUNK], F32, name=f"h_bank{c}", tag=f"hy{c}")
+            h_bank = psum.tile([P, PACK, CHUNK], F32, name=f"h_bank{c}", tag=f"hy{c}")
             for t in range(PACK):
-                product(bank[:, t, :], "w3", t, "now", tokens, True, False)
-                product(bank[:, t, :], "w4", t, "prev", tokens, False, True)
-            nc.scalar.activation(h_rounded[:, PACK * CHUNK * c : PACK * CHUNK * (c + 1)].rearrange("p (n t) -> p n t", t=PACK),
-                                 bank[:].rearrange("p t n -> p n t"), ACT.Relu)
+                product(h_bank[:, t, :], "w3", t, "now", tokens, True, False)
+                product(h_bank[:, t, :], "w4", t, "prev", tokens, False, True)
+            nc.scalar.activation(
+                h_rounded[:, PACK * CHUNK * c : PACK * CHUNK * (c + 1)].rearrange("p (n t) -> p n t", t=PACK),
+                h_bank[:].rearrange("p t n -> p n t"),
+                ACT.Relu,
+            )
 
         z_banks = [psum.tile([P, S], F32, name=f"z_bank{t}", tag=f"z{t}") for t in range(PACK)]
         for t in range(PACK):
-            product(z_banks[t][:], "w1", t, "now", everyone, True, False)
+            product(z_banks[t][:], "w1", t, "now", all_tokens, True, False)
 
-        round_weight(on_vector, "w2", 0, 1)
-        round_weight(on_vector, "w2", 1, 2)
+        round_weight(on_vector, "w2", 0)
+        round_weight(on_vector, "w2", 1)
         words["h"] = keep.tile([P, S], U32, name="words_h", tag="raw_w2", align_bytes=64)
         scales["h"] = keep.tile([P, S], U8, name="scales_h", align_bytes=64)
-        quantize("w2", rounded["w2"], 0, N // 2)
+        quantize("w2", rounded["w2"], 0, pair)
         quantize("h", h_rounded, 0, HALF)
-        quantize("w2", rounded["w2"], N // 2, N // 2)
+        quantize("w2", rounded["w2"], pair, pair)
         quantize("h", h_rounded, HALF, HALF)
         for t in range(PACK):
-            product(z_banks[t][:], "w2", t, "prev", everyone, False, True)
+            product(z_banks[t][:], "w2", t, "prev", all_tokens, False, True)
 
-        round_weight(on_scalar, "w5", 1, 2)
-        round_weight(on_vector, "w5", 0, 1)
-        quantize("w5", rounded["w5"], 0, N // 2)
-        quantize("w5", rounded["w5"], N // 2, N // 2)
+        round_weight(on_scalar, "w5", 1)
+        round_weight(on_vector, "w5", 0)
+        quantize("w5", rounded["w5"], 0, P)
+        quantize("w5", rounded["w5"], P, P)
+        quantize("w5", rounded["w5"], pair, pair)
 
         gate = keep.tile([P, PACK, S], F32, name="gate", tag="raw_w5", align_bytes=64)
         result = keep.tile([P, PACK, S], F32, name="result", align_bytes=64)
         out_rows = out_0.rearrange("(p t) n -> p t n", t=PACK)
         for t in range(PACK):
             nc.scalar.activation(gate[:, t, :], z_banks[t][:], ACT.Sigmoid)
-            bank = psum.tile([P, S], F32, name=f"y_bank{t}", tag=f"hy{t}")
-            product(bank[:], "w5", t, "h", everyone, True, True)
-            for tokens in ([everyone] if t < PACK - 1 else [slice(0, HALF), slice(HALF, S)]):
-                nc.vector.tensor_tensor(result[:, t, tokens], bank[:, tokens], gate[:, t, tokens], ALU.mult)
+            y_bank = psum.tile([P, S], F32, name=f"y_bank{t}", tag=f"hy{t}")
+            product(y_bank[:], "w5", t, "h", all_tokens, True, True)
+            last_slot = t == PACK - 1
+            for tokens in [slice(0, HALF), slice(HALF, S)] if last_slot else [all_tokens]:
+                nc.vector.tensor_tensor(result[:, t, tokens], y_bank[:, tokens], gate[:, t, tokens], ALU.mult)
             nc.sync.dma_start(out_rows[:, t, :], result[:, t, :])
 
         result_rounded = keep.tile([P, S * PACK], BF16, name="result_rounded", align_bytes=64)
@@ -153,6 +167,6 @@ def tile_picked_zshift_relu_po_kernel(tc, x_words, x_scales, w1, w2, w3, w4, w5,
         for first in (0, HALF):
             quantize("out", result_rounded, first, HALF)
             nc.sync.dma_start(out_words[:, first : first + HALF], words["out"][:, first : first + HALF].bitcast(I32))
-        for r in range(4):
+        for r in range(PACK):
             queue = nc.sync if r % 2 == 0 else nc.scalar
-            queue.dma_start(out_2[0, r:16:4, :].bitcast(I32), scales["out"][r:P:32, :].bitcast(I32))
+            queue.dma_start(out_2[0, r:SCALE_ROWS:PACK, :].bitcast(I32), scales["out"][r:P:QUADRANT, :].bitcast(I32))

from contextlib import ExitStack

import concourse.mybir as mybir

T, S, N = 1024, 512, 512
FLOPS = 5 * 2 * 512 * 512 * 512

F32 = mybir.dt.float32
BF16 = mybir.dt.bfloat16
I32 = mybir.dt.int32
U32 = mybir.dt.uint32
U16 = mybir.dt.uint16
U8 = mybir.dt.uint8
FP8X4 = mybir.dt.float8_e4m3fn_x4
ACT = mybir.ActivationFunctionType
ALU = mybir.AluOpType

P = 128
PACK = 4
QUADRANT = 32
SCALE_ROWS = 16
CHUNK = 128
HALF = S // 2
SCALAR_TAIL = 64


def tile_picked_zshift_relu_po_kernel(tc, x_words, x_scales, w1, w2, w3, w4, w5, offs, prev, out_0, out_1, out_2):
    nc = tc.nc
    with ExitStack() as ctx:
        keep = ctx.enter_context(tc.tile_pool(name="keep", bufs=1))
        psum = ctx.enter_context(tc.psum_pool(name="psum", bufs=1))

        offs_sb = keep.tile([P, S // 16], U16, name="offs_sb")
        prev_sb = keep.tile([P, S // 16], U16, name="prev_sb")
        table_words = keep.tile([P, T], I32, name="table_words", align_bytes=64)
        table_scales = keep.tile([P, T], U8, name="table_scales", align_bytes=64)
        nc.vector.memset(table_scales[:].bitcast(I32), 0)
        nc.sync.dma_start(table_words[:], x_words[0].rearrange("p c r -> p (c r)").bitcast(I32))
        nc.sync.dma_start(offs_sb[:], offs)
        for r in range(PACK):
            nc.sync.dma_start(table_scales[r:P:QUADRANT, :].bitcast(I32), x_scales[0, r:SCALE_ROWS:PACK, :].bitcast(I32))
        nc.sync.dma_start(prev_sb[:], prev)

        preload_in = keep.tile([P, 8], F32, name="preload_in")
        preload_out = keep.tile([P, 8], F32, name="preload_out")
        nc.vector.memset(preload_in[:], 0.0)
        nc.scalar.activation(preload_out[:], preload_in[:], ACT.Sigmoid)

        weights = {"w3": w3, "w4": w4, "w1": w1, "w2": w2, "w5": w5}
        raw = {}
        for name, w in weights.items():
            raw[name] = keep.tile([P, PACK, N], F32, name=f"raw_{name}", tag=f"raw_{name}", align_bytes=64)
            nc.sync.dma_start(raw[name][:], w.rearrange("(p j) m -> p j m", j=PACK))

        words, scales = {}, {}
        for name, offsets in (("now", offs_sb), ("prev", prev_sb)):
            words[name] = keep.tile([P, S], U32, name=f"words_{name}", align_bytes=64)
            nc.vector.tensor_copy(words[name][:], table_words[:].bitcast(U32).indirect(offsets[:]))
        for name, offsets in (("now", offs_sb), ("prev", prev_sb)):
            scales[name] = keep.tile([P, S], U8, name=f"scales_{name}", align_bytes=64)
            nc.vector.tensor_copy(scales[name][:], table_scales[:].indirect(offsets[:]))

        rounded = {}
        for name in weights:
            rounded[name] = keep.tile([P, PACK * N], BF16, name=f"rounded_{name}", align_bytes=64)
            words[name] = keep.tile([P, N], U32, name=f"words_{name}", align_bytes=64)
            scales[name] = keep.tile([P, N], U8, name=f"scales_{name}", align_bytes=64)

        def round_weight(copy, name, u):
            src = raw[name][:].rearrange("p j (m u e) -> p u m j e", u=2, e=2)[:, u : u + 1]
            dst = rounded[name][:].rearrange("p (u e m j) -> p u m j e", u=2, e=2, j=PACK)[:, u : u + 1]
            copy(dst, src)

        def quantize(name, source, first, count):
            cols = slice(first, first + count)
            nc.vector.quantize_mx(
                out=words[name][:, cols].bitcast(FP8X4),
                scales=scales[name][:, cols],
                in_=source[:, PACK * first : PACK * (first + count)],
            )

        def product(out, weight, t, moving, tokens, start, stop):
            cols = slice(P * t, P * t + P)
            nc.tensor.matmul_mx(
                out=out,
                lhsT=words[weight][:, cols].bitcast(FP8X4),
                lhsT_scale=scales[weight][:, cols],
                rhs=words[moving][:, tokens].bitcast(FP8X4),
                rhs_scale=scales[moving][:, tokens],
                start=start,
                stop=stop,
            )

        on_scalar, on_vector = nc.scalar.copy, nc.vector.tensor_copy
        all_tokens = slice(0, S)
        pair = N // 2

        round_weight(on_scalar, "w3", 1)
        round_weight(on_scalar, "w3", 0)
        quantize("w3", rounded["w3"], pair, pair)
        quantize("w3", rounded["w3"], 0, pair)
        for name in ("w4", "w1"):
            round_weight(on_scalar, name, 1)
            round_weight(on_vector, name, 0)
            quantize(name, rounded[name], 0, N)

        h_rounded = keep.tile([P, S * PACK], BF16, name="h_rounded", tag="raw_w1", align_bytes=64)
        for c in range(S // CHUNK):
            tokens = slice(CHUNK * c, CHUNK * c + CHUNK)
            h_bank = psum.tile([P, PACK, CHUNK], F32, name=f"h_bank{c}", tag=f"hy{c}")
            for t in range(PACK):
                product(h_bank[:, t, :], "w3", t, "now", tokens, True, False)
                product(h_bank[:, t, :], "w4", t, "prev", tokens, False, True)
            nc.scalar.activation(
                h_rounded[:, PACK * CHUNK * c : PACK * CHUNK * (c + 1)].rearrange("p (n t) -> p n t", t=PACK),
                h_bank[:].rearrange("p t n -> p n t"),
                ACT.Relu,
            )

        z_banks = [psum.tile([P, S], F32, name=f"z_bank{t}", tag=f"z{t}") for t in range(PACK)]
        for t in range(PACK):
            product(z_banks[t][:], "w1", t, "now", all_tokens, True, False)

        round_weight(on_vector, "w2", 0)
        round_weight(on_vector, "w2", 1)
        words["h"] = keep.tile([P, S], U32, name="words_h", tag="raw_w2", align_bytes=64)
        scales["h"] = keep.tile([P, S], U8, name="scales_h", align_bytes=64)
        quantize("w2", rounded["w2"], 0, pair)
        quantize("h", h_rounded, 0, HALF)
        quantize("w2", rounded["w2"], pair, pair)
        quantize("h", h_rounded, HALF, HALF)
        for t in range(PACK):
            product(z_banks[t][:], "w2", t, "prev", all_tokens, False, True)

        round_weight(on_scalar, "w5", 1)
        round_weight(on_vector, "w5", 0)
        quantize("w5", rounded["w5"], 0, P)
        quantize("w5", rounded["w5"], P, P)
        quantize("w5", rounded["w5"], pair, pair)

        gate = keep.tile([P, PACK, S], F32, name="gate", tag="raw_w5", align_bytes=64)
        result = keep.tile([P, PACK, S], F32, name="result", align_bytes=64)
        out_rows = out_0.rearrange("(p t) n -> p t n", t=PACK)
        for t in range(PACK):
            nc.scalar.activation(gate[:, t, :], z_banks[t][:], ACT.Sigmoid)
            y_bank = psum.tile([P, S], F32, name=f"y_bank{t}", tag=f"hy{t}")
            product(y_bank[:], "w5", t, "h", all_tokens, True, True)
            last_slot = t == PACK - 1
            for tokens in [slice(0, HALF), slice(HALF, S)] if last_slot else [all_tokens]:
                nc.vector.tensor_tensor(result[:, t, tokens], y_bank[:, tokens], gate[:, t, tokens], ALU.mult)
            nc.sync.dma_start(out_rows[:, t, :], result[:, t, :])

        result_rounded = keep.tile([P, S * PACK], BF16, name="result_rounded", align_bytes=64)
        words["out"] = keep.tile([P, S], U32, name="words_out", align_bytes=64)
        scales["out"] = keep.tile([P, S], U8, name="scales_out", align_bytes=64)

        def round_result(copy, first, last):
            src = result[:, :, first:last].rearrange("p t (a i) -> p a t i", i=4)
            dst = result_rounded[:, PACK * first : PACK * last].rearrange("p (a i t) -> p a t i", i=4, t=PACK)
            copy(dst, src)

        round_result(on_scalar, 0, CHUNK)
        round_result(on_vector, CHUNK, HALF)
        round_result(on_vector, HALF, S - SCALAR_TAIL)
        round_result(on_scalar, S - SCALAR_TAIL, S)
        out_words = out_1[0].rearrange("p c r -> p (c r)").bitcast(I32)
        for first in (0, HALF):
            quantize("out", result_rounded, first, HALF)
            nc.sync.dma_start(out_words[:, first : first + HALF], words["out"][:, first : first + HALF].bitcast(I32))
        for r in range(PACK):
            queue = nc.sync if r % 2 == 0 else nc.scalar
            queue.dma_start(out_2[0, r:SCALE_ROWS:PACK, :].bitcast(I32), scales["out"][r:P:QUADRANT, :].bitcast(I32))
